import numpy as np
import ml_dtypes


def mxq(x, axis, fmt="e4m3"):
    dtype, down = {"e4m3": (ml_dtypes.float8_e4m3fn, 7), "e5m2": (ml_dtypes.float8_e5m2, 14)}[fmt]
    v = np.moveaxis(np.asarray(x, np.float32).astype(ml_dtypes.bfloat16).astype(np.float64), axis, -1)
    blocks = v.reshape(v.shape[:-1] + (-1, 32))
    amax = np.abs(blocks).max(-1, keepdims=True)
    byte = np.maximum(np.where(amax > 0, np.frexp(amax)[1] - 1 + 127, 0) - down, 1)
    scale = np.exp2(byte - 127.0)
    codes = (blocks / scale).astype(np.float32).astype(dtype).astype(np.float64)
    return np.moveaxis((codes * scale).reshape(v.shape), -1, axis)


WIDE = False


def mx_kscale(k):
    if not WIDE:
        return np.ones(k)
    levels = np.array([10, -10, 5, -5, 0])
    if k % 512:
        return np.exp2(np.random.permutation(np.resize(levels, k // 32))).repeat(32)
    a = np.empty((k // 512, 16))
    for p in range(k // 512):
        a[p, :8] = np.random.permutation(np.resize(levels, 8))
        for g in range(8):
            far = levels[np.abs(levels - a[p, g]) >= 10]
            a[p, g + 8] = far[np.random.randint(len(far))]
    return np.exp2(a.ravel()).repeat(32)


def f64(x):
    return np.asarray(x).astype(np.float64)


def striped8(idx):
    return np.asarray(idx).reshape(8, -1, 16).transpose(0, 2, 1).reshape(128, -1).astype(np.uint16)


def unstriped8(offs):
    return offs.reshape(8, 16, -1).transpose(0, 2, 1).reshape(8, -1).astype(np.int64)


def pick8(x, idx, run):
    r = np.arange(len(x))
    return x[r[:, None], idx[r % (8 * run) // run]]


E2M1 = np.array([0.0, 0.5, 1.0, 1.5, 2.0, 3.0, 4.0, 6.0, -0.0, -0.5, -1.0, -1.5, -2.0, -3.0, -4.0, -6.0])


def pack_weight(w, fmt):
    k, n = w.shape
    w = f64(np.asarray(w, np.float32).astype(ml_dtypes.bfloat16)).reshape(k // 32, 32, n)
    amax = np.abs(w).max(1)
    if fmt == "e4m3":
        byte = np.frexp(amax)[1] - 1 + 127 - 7
    else:
        mant, ex = np.frexp(amax / 6.0)
        byte = np.where(mant > 0.5, ex, ex - 1) + 127
    byte = np.clip(np.where(amax > 0, byte, 1), 1, 254)
    scaled = (w * np.exp2(127.0 - byte)[:, None, :]).reshape(k, n).astype(np.float32)
    by_word = np.ascontiguousarray(scaled.reshape(k // 512, 128, 4, n).transpose(0, 1, 3, 2))
    if fmt == "e4m3":
        words = by_word.astype(ml_dtypes.float8_e4m3fn).view(np.uint8)
    else:
        c = by_word.astype(ml_dtypes.float4_e2m1fn).view(np.uint8) & 0xF
        words = (c[..., 0::2] | (c[..., 1::2] << 4)).reshape(k // 512, 128, 2 * n)
    return np.ascontiguousarray(words), np.ascontiguousarray(byte.astype(np.uint8).reshape(k // 512, 16, n))


def unpack_weight(words, scales, fmt):
    g, _, n = scales.shape
    words = np.ascontiguousarray(words).reshape(g, 128, n, -1)
    if fmt == "e4m3":
        vals = words.view(ml_dtypes.float8_e4m3fn).astype(np.float64)
    else:
        nib = np.empty((g, 128, n, 4), np.uint8)
        nib[..., 0::2] = words & 0xF
        nib[..., 1::2] = words >> 4
        vals = E2M1[nib]
    vals = vals * np.repeat(np.exp2(scales.astype(np.float64) - 127.0), 8, axis=1)[..., None]
    return vals.transpose(0, 1, 3, 2).reshape(g * 512, n)


D, T, I, Q = 512, 1024, 512, 128


def setup_inputs():
    n = np.random.standard_normal
    idx = np.stack([np.random.permutation(T)[:I] for _ in range(8)])
    idx2 = np.stack([np.random.permutation(T)[:I] for _ in range(8)])
    idx3 = np.stack([np.random.permutation(T)[:I] for _ in range(8)])
    fd = mx_kscale(D)
    keysp = pack_weight(n((D, T)) / fd[:, None], "e4m3")
    return {
        "query": (n((D, Q)) * 0.9 / np.sqrt(D) * fd[:, None]).astype(np.float32),
        "query2": (n((D, Q)) * 0.9 / np.sqrt(D) * fd[:, None]).astype(np.float32),
        "keys_words": keysp[0],
        "keys_scales": keysp[1],
        "lam": (np.random.uniform(0.5, 1.3, (Q, 1))).astype(np.float32),
        "old": (1.0 * n((Q, T))).astype(np.float32),
        "offs": striped8(idx),
        "offs2": striped8(idx2),
        "offs3": striped8(idx3),
    }


def reference(query, query2, keys_words, keys_scales, lam, old, offs, offs2, offs3):
    idx = unstriped8(offs)
    idx2 = unstriped8(offs2)
    idx3 = unstriped8(offs3)
    keysu = unpack_weight(keys_words, keys_scales, "e4m3")
    queryq = mxq(f64(query), 0, "e4m3")
    a = queryq.T @ keysu
    query2q = mxq(f64(query2), 0, "e4m3")
    b = query2q.T @ keysu
    w = (np.maximum(pick8(a, idx, 16), pick8(b, idx2, 16)) - np.maximum(pick8(a, idx2, 16), pick8(b, idx, 16))) * f64(lam)
    f1 = np.zeros((Q, T))
    f1[np.arange(Q)[:, None], idx[np.arange(Q) % 128 // 16]] = w
    f2 = f1 + f64(old)
    y = pick8(f2, idx3, 16)
    return y

@@ -1,0 +1,139 @@
+from contextlib import ExitStack
+
+import concourse.mybir as mybir
+
+D, T, I, Q = 512, 1024, 512, 128
+FLOPS = 2 * 2 * D * Q * T
+
+F32 = mybir.dt.float32
+BF16 = mybir.dt.bfloat16
+I32 = mybir.dt.int32
+U32 = mybir.dt.uint32
+U16 = mybir.dt.uint16
+U8 = mybir.dt.uint8
+FP8X4 = mybir.dt.float8_e4m3fn_x4
+ALU = mybir.AluOpType
+COPY = mybir.ActivationFunctionType.Copy
+
+P = 128
+PACK = 4
+N_PASS = 256
+HALF = 256
+PIECE = 128
+
+
+def tile_attend_exchanged_lean_through_heads_kernel(
+    tc, query, query2, keys_words, keys_scales, lam, old, offs, offs2, offs3, out
+):
+    nc = tc.nc
+    with ExitStack() as ctx:
+        sb = ctx.enter_context(tc.tile_pool(name="sb", bufs=1))
+        ps = ctx.enter_context(tc.psum_pool(name="ps", bufs=1))
+
+        list1 = sb.tile([P, I // 16], U16, name="list1")
+        list2 = sb.tile([P, I // 16], U16, name="list2")
+        list3 = sb.tile([P, I // 16], U16, name="list3")
+
+        key_scale = sb.tile([P, T], U8, name="key_scale", align_bytes=64)
+        nc.vector.memset(key_scale[:].bitcast(I32), 0)
+        f1 = sb.tile([P, T], F32, name="f1")
+        nc.vector.memset(f1[:], 0.0)
+
+        raw = [sb.tile([P, PACK, Q], F32, name=f"raw{s}", tag=f"stage{s}") for s in range(2)]
+        key_words = [sb.tile([P, T // 2], U32, name=f"key_words{h}", align_bytes=64) for h in range(2)]
+        words_hbm = keys_words[0].rearrange("p n t -> p (n t)")
+        half_bytes = PACK * T // 2
+
+        lam_col = sb.tile([P, 1], F32, name="lam_col")
+        nc.gpsimd.dma_start(out=lam_col[:], in_=lam)
+
+        nc.sync.dma_start(out=raw[0][:], in_=query.rearrange("(p j) w -> p j w", j=PACK))
+        for quad in range(4):
+            nc.sync.dma_start(
+                out=key_scale[32 * quad : 32 * quad + 4, :].bitcast(I32),
+                in_=keys_scales[0, 4 * quad : 4 * quad + 4, :].bitcast(I32),
+            )
+        nc.sync.dma_start(out=key_words[0][:].bitcast(I32), in_=words_hbm[:, 0:half_bytes].bitcast(I32))
+        nc.sync.dma_start(out=raw[1][:], in_=query2.rearrange("(p j) w -> p j w", j=PACK))
+        nc.sync.dma_start(out=key_words[1][:].bitcast(I32), in_=words_hbm[:, half_bytes:].bitcast(I32))
+        nc.sync.dma_start(list1[:], offs)
+        nc.sync.dma_start(list2[:], offs2)
+        nc.sync.dma_start(list3[:], offs3)
+
+        lam_wide = sb.tile([P, HALF], F32, name="lam_wide")
+        nc.gpsimd.tensor_scalar(lam_wide[:], lam_col[:, 0:1].to_broadcast([P, HALF]), 1.0, 0.0, ALU.mult, ALU.add)
+
+        scores = []
+        for s in range(2):
+            grouped = sb.tile([P, Q, PACK], BF16, name=f"grouped{s}", align_bytes=64)
+            nc.vector.tensor_copy(
+                out=grouped[:].rearrange("p (c i) t -> p c t i", i=4),
+                in_=raw[s][:].rearrange("p t (c i) -> p c t i", i=4),
+            )
+            codes = sb.tile([P, Q], U32, name=f"codes{s}", align_bytes=64)
+            scale = sb.tile([P, Q], U8, name=f"scale{s}", align_bytes=64)
+            nc.vector.quantize_mx(
+                out=codes[:].bitcast(FP8X4), scales=scale[:], in_=grouped[:].rearrange("p w j -> p (w j)")
+            )
+            score = sb.tile([P, T], F32, name=f"score{s}")
+            scores.append(score)
+            for n in range(T // N_PASS):
+                cols = slice(n * N_PASS, (n + 1) * N_PASS)
+                h, c0 = divmod(n * N_PASS, T // 2)
+                bank = ps.tile([P, N_PASS], F32, name=f"bank{s}_{n}")
+                nc.tensor.matmul_mx(
+                    out=bank[:],
+                    lhsT=codes[:].bitcast(FP8X4),
+                    lhsT_scale=scale[:],
+                    rhs=key_words[h][:, c0 : c0 + N_PASS].bitcast(FP8X4),
+                    rhs_scale=key_scale[:, cols],
+                    start=True,
+                    stop=True,
+                )
+                if s == 0 and n < 3:
+                    nc.scalar.activation(score[:, cols], bank[:], COPY)
+                else:
+                    nc.vector.tensor_copy(out=score[:, cols], in_=bank[:])
+        a, b = scores
+        old_sb = sb.tile([P, T], F32, name="old_sb", tag="stage1")
+        nc.sync.dma_start(out=old_sb[:], in_=old)
+
+        def entries(lst, start, count):
+            return lst[:, start // 16 : (start + count) // 16]
+
+        ga = sb.tile([P, 2, HALF], F32, name="ga")
+        gb = [sb.tile([P, 2, HALF], F32, name=f"gb{c}") for c in range(2)]
+        top = [sb.tile([P, 2, HALF], F32, name=f"top{c}") for c in range(2)]
+
+        def look_scalar(dst, window, lst, c):
+            nc.scalar.activation(dst, window[:].indirect(entries(lst, c * HALF, HALF)), COPY)
+
+        for c in range(2):
+            if c == 0:
+                look_scalar(ga[:, 0, :], a, list1, c)
+                look_scalar(ga[:, 1, :], a, list2, c)
+                look_scalar(gb[c][:, 1, :], b, list1, c)
+                nc.vector.tensor_copy(gb[c][:, 0, :], b[:].indirect(entries(list2, 0, HALF)))
+                look_scalar(gb[1][:, 0, :], b, list2, 1)
+                look_scalar(gb[1][:, 1, :], b, list1, 1)
+            else:
+                look_scalar(ga[:, 0, :], a, list1, c)
+                look_scalar(ga[:, 1, :], a, list2, c)
+            for p in range(2):
+                cols = slice(p * PIECE, (p + 1) * PIECE)
+                nc.vector.tensor_tensor(top[c][:, :, cols], ga[:, :, cols], gb[c][:, :, cols], ALU.max)
+            for p in range(2):
+                cols = slice(p * PIECE, (p + 1) * PIECE)
+                nc.vector.tensor_tensor(top[c][:, 0, cols], top[c][:, 0, cols], top[c][:, 1, cols], ALU.subtract)
+            nc.vector.tensor_tensor(
+                f1[:].indirect(entries(list1, c * HALF, HALF)), top[c][:, 0, :], lam_wide[:], ALU.mult
+            )
+
+        f2 = sb.tile([P, T], F32, name="f2")
+        nc.vector.tensor_tensor(f2[:], f1[:], old_sb[:], ALU.add)
+
+        res = [sb.tile([P, HALF], F32, name=f"res{c}") for c in range(2)]
+        nc.vector.tensor_copy(res[0][:], f2[:].indirect(entries(list3, 0, HALF)))
+        nc.sync.dma_start(out=out[:, 0:HALF], in_=res[0][:])
+        look_scalar(res[1][:], f2, list3, 1)
+        nc.scalar.dma_start(out=out[:, HALF:], in_=res[1][:])

@@ -44,32 +44,36 @@ def tile_attend_exchanged_lean_through_heads_kernel(
         words_hbm = keys_words[0].rearrange("p n t -> p (n t)")
         half_bytes = PACK * T // 2
 
-        lam_col = sb.tile([P, 1], F32, name="lam_col")
-        nc.gpsimd.dma_start(out=lam_col[:], in_=lam)
-
         nc.sync.dma_start(out=raw[0][:], in_=query.rearrange("(p j) w -> p j w", j=PACK))
+        nc.sync.dma_start(out=key_words[0][:].bitcast(I32), in_=words_hbm[:, 0:half_bytes].bitcast(I32))
         for quad in range(4):
             nc.sync.dma_start(
                 out=key_scale[32 * quad : 32 * quad + 4, :].bitcast(I32),
                 in_=keys_scales[0, 4 * quad : 4 * quad + 4, :].bitcast(I32),
             )
-        nc.sync.dma_start(out=key_words[0][:].bitcast(I32), in_=words_hbm[:, 0:half_bytes].bitcast(I32))
         nc.sync.dma_start(out=raw[1][:], in_=query2.rearrange("(p j) w -> p j w", j=PACK))
         nc.sync.dma_start(out=key_words[1][:].bitcast(I32), in_=words_hbm[:, half_bytes:].bitcast(I32))
         nc.sync.dma_start(list1[:], offs)
         nc.sync.dma_start(list2[:], offs2)
         nc.sync.dma_start(list3[:], offs3)
+        lam_col = sb.tile([P, 1], F32, name="lam_col")
+        nc.sync.dma_start(out=lam_col[:], in_=lam)
 
-        lam_wide = sb.tile([P, HALF], F32, name="lam_wide")
-        nc.gpsimd.tensor_scalar(lam_wide[:], lam_col[:, 0:1].to_broadcast([P, HALF]), 1.0, 0.0, ALU.mult, ALU.add)
+        lam_wide = sb.tile([P, PIECE], F32, name="lam_wide")
+        nc.gpsimd.tensor_scalar(lam_wide[:], lam_col[:, 0:1].to_broadcast([P, PIECE]), 1.0, 0.0, ALU.mult, ALU.add)
+        lam_neg = sb.tile([P, 1], F32, name="lam_neg")
+        nc.gpsimd.tensor_scalar(lam_neg[:], lam_col[:], -1.0, 0.0, ALU.mult, ALU.add)
 
         scores = []
         for s in range(2):
             grouped = sb.tile([P, Q, PACK], BF16, name=f"grouped{s}", align_bytes=64)
-            nc.vector.tensor_copy(
-                out=grouped[:].rearrange("p (c i) t -> p c t i", i=4),
-                in_=raw[s][:].rearrange("p t (c i) -> p c t i", i=4),
-            )
+            dst = grouped[:].rearrange("p (c i) t -> p c t i", i=4)
+            src = raw[s][:].rearrange("p t (c i) -> p c t i", i=4)
+            if s == 0:
+                nc.vector.tensor_copy(out=dst[:, :16], in_=src[:, :16])
+                nc.scalar.activation(dst[:, 16:], src[:, 16:], COPY)
+            else:
+                nc.vector.tensor_copy(out=dst, in_=src)
             codes = sb.tile([P, Q], U32, name=f"codes{s}", align_bytes=64)
             scale = sb.tile([P, Q], U8, name=f"scale{s}", align_bytes=64)
             nc.vector.quantize_mx(
@@ -77,10 +81,10 @@ def tile_attend_exchanged_lean_through_heads_kernel(
             )
             score = sb.tile([P, T], F32, name=f"score{s}")
             scores.append(score)
-            for n in range(T // N_PASS):
+            for n in (0, 1, 2, 3) if s == 0 else (2, 3, 0, 1):
                 cols = slice(n * N_PASS, (n + 1) * N_PASS)
                 h, c0 = divmod(n * N_PASS, T // 2)
-                bank = ps.tile([P, N_PASS], F32, name=f"bank{s}_{n}")
+                bank = ps.tile([P, N_PASS], F32, name=f"bank{s}_{n}", tag=f"bank{n + 2 * s if s == 0 or n < 2 else n + 2}")
                 nc.tensor.matmul_mx(
                     out=bank[:],
                     lhsT=codes[:].bitcast(FP8X4),
@@ -101,33 +105,39 @@ def tile_attend_exchanged_lean_through_heads_kernel(
         def entries(lst, start, count):
             return lst[:, start // 16 : (start + count) // 16]
 
-        ga = sb.tile([P, 2, HALF], F32, name="ga")
-        gb = [sb.tile([P, 2, HALF], F32, name=f"gb{c}") for c in range(2)]
-        top = [sb.tile([P, 2, HALF], F32, name=f"top{c}") for c in range(2)]
+        ga = sb.tile([P, 2 * HALF], F32, name="ga")
+        gb = [sb.tile([P, 2 * HALF], F32, name=f"gb{c}") for c in range(2)]
+        top = sb.tile([P, 2, HALF], F32, name="top")
+        late = [sb.tile([P, HALF], F32, name=f"late{s}") for s in range(2)]
+        term = [sb.tile([P, HALF], F32, name=f"term{s}") for s in range(2)]
+
+        def pairs(tile):
+            return tile[:].rearrange("p (s i) -> p s i", s=2)
 
         def look_scalar(dst, window, lst, c):
             nc.scalar.activation(dst, window[:].indirect(entries(lst, c * HALF, HALF)), COPY)
 
-        for c in range(2):
-            if c == 0:
-                look_scalar(ga[:, 0, :], a, list1, c)
-                look_scalar(ga[:, 1, :], a, list2, c)
-                look_scalar(gb[c][:, 1, :], b, list1, c)
-                nc.vector.tensor_copy(gb[c][:, 0, :], b[:].indirect(entries(list2, 0, HALF)))
-                look_scalar(gb[1][:, 0, :], b, list2, 1)
-                look_scalar(gb[1][:, 1, :], b, list1, 1)
-            else:
-                look_scalar(ga[:, 0, :], a, list1, c)
-                look_scalar(ga[:, 1, :], a, list2, c)
-            for p in range(2):
-                cols = slice(p * PIECE, (p + 1) * PIECE)
-                nc.vector.tensor_tensor(top[c][:, :, cols], ga[:, :, cols], gb[c][:, :, cols], ALU.max)
-            for p in range(2):
-                cols = slice(p * PIECE, (p + 1) * PIECE)
-                nc.vector.tensor_tensor(top[c][:, 0, cols], top[c][:, 0, cols], top[c][:, 1, cols], ALU.subtract)
+        look_scalar(ga[:, :HALF], a, list1, 0)
+        look_scalar(ga[:, HALF:], a, list2, 0)
+        look_scalar(gb[0][:, HALF:], b, list1, 0)
+        nc.vector.tensor_copy(gb[0][:, :HALF], b[:].indirect(entries(list2, 0, HALF)))
+        look_scalar(gb[1][:, :HALF], b, list2, 1)
+        look_scalar(gb[1][:, HALF:], b, list1, 1)
+        pieces = [slice(p * PIECE, (p + 1) * PIECE) for p in range(2)]
+        for cols in pieces:
+            nc.vector.tensor_tensor(top[:, :, cols], pairs(ga)[:, :, cols], pairs(gb[0])[:, :, cols], ALU.max)
+        for cols in pieces:
+            nc.vector.tensor_tensor(top[:, 0, cols], top[:, 0, cols], top[:, 1, cols], ALU.subtract)
+        look_scalar(ga[:, :HALF], a, list1, 1)
+        look_scalar(ga[:, HALF:], a, list2, 1)
+        for p, (cols, factor) in enumerate(zip(pieces, (lam_col, lam_neg))):
             nc.vector.tensor_tensor(
-                f1[:].indirect(entries(list1, c * HALF, HALF)), top[c][:, 0, :], lam_wide[:], ALU.mult
+                f1[:].indirect(entries(list1, p * PIECE, PIECE)), top[:, 0, cols], lam_wide[:], ALU.mult
             )
+            for part in [slice(0, HALF)] if p == 0 else pieces:
+                nc.vector.tensor_tensor(late[p][:, part], pairs(ga)[:, p, part], pairs(gb[1])[:, p, part], ALU.max)
+                nc.scalar.activation(term[p][:, part], late[p][:, part], COPY, scale=factor[:, 0:1])
+        nc.vector.tensor_tensor(f1[:].indirect(entries(list1, HALF, HALF)), term[0][:], term[1][:], ALU.add)
 
         f2 = sb.tile([P, T], F32, name="f2")
         nc.vector.tensor_tensor(f2[:], f1[:], old_sb[:], ALU.add)

from contextlib import ExitStack

import concourse.mybir as mybir

D, T, I, Q = 512, 1024, 512, 128
FLOPS = 2 * 2 * D * Q * T

F32 = mybir.dt.float32
BF16 = mybir.dt.bfloat16
I32 = mybir.dt.int32
U32 = mybir.dt.uint32
U16 = mybir.dt.uint16
U8 = mybir.dt.uint8
FP8X4 = mybir.dt.float8_e4m3fn_x4
ALU = mybir.AluOpType
COPY = mybir.ActivationFunctionType.Copy

P = 128
PACK = 4
N_PASS = 256
HALF = 256
PIECE = 128


def tile_attend_exchanged_lean_through_heads_kernel(
    tc, query, query2, keys_words, keys_scales, lam, old, offs, offs2, offs3, out
):
    nc = tc.nc
    with ExitStack() as ctx:
        sb = ctx.enter_context(tc.tile_pool(name="sb", bufs=1))
        ps = ctx.enter_context(tc.psum_pool(name="ps", bufs=1))

        list1 = sb.tile([P, I // 16], U16, name="list1")
        list2 = sb.tile([P, I // 16], U16, name="list2")
        list3 = sb.tile([P, I // 16], U16, name="list3")

        key_scale = sb.tile([P, T], U8, name="key_scale", align_bytes=64)
        nc.vector.memset(key_scale[:].bitcast(I32), 0)
        f1 = sb.tile([P, T], F32, name="f1")
        nc.vector.memset(f1[:], 0.0)

        raw = [sb.tile([P, PACK, Q], F32, name=f"raw{s}", tag=f"stage{s}") for s in range(2)]
        key_words = [sb.tile([P, T // 2], U32, name=f"key_words{h}", align_bytes=64) for h in range(2)]
        words_hbm = keys_words[0].rearrange("p n t -> p (n t)")
        half_bytes = PACK * T // 2

        nc.sync.dma_start(out=raw[0][:], in_=query.rearrange("(p j) w -> p j w", j=PACK))
        nc.sync.dma_start(out=key_words[0][:].bitcast(I32), in_=words_hbm[:, 0:half_bytes].bitcast(I32))
        for quad in range(4):
            nc.sync.dma_start(
                out=key_scale[32 * quad : 32 * quad + 4, :].bitcast(I32),
                in_=keys_scales[0, 4 * quad : 4 * quad + 4, :].bitcast(I32),
            )
        nc.sync.dma_start(out=raw[1][:], in_=query2.rearrange("(p j) w -> p j w", j=PACK))
        nc.sync.dma_start(out=key_words[1][:].bitcast(I32), in_=words_hbm[:, half_bytes:].bitcast(I32))
        nc.sync.dma_start(list1[:], offs)
        nc.sync.dma_start(list2[:], offs2)
        nc.sync.dma_start(list3[:], offs3)
        lam_col = sb.tile([P, 1], F32, name="lam_col")
        nc.sync.dma_start(out=lam_col[:], in_=lam)

        lam_wide = sb.tile([P, PIECE], F32, name="lam_wide")
        nc.gpsimd.tensor_scalar(lam_wide[:], lam_col[:, 0:1].to_broadcast([P, PIECE]), 1.0, 0.0, ALU.mult, ALU.add)
        lam_neg = sb.tile([P, 1], F32, name="lam_neg")
        nc.gpsimd.tensor_scalar(lam_neg[:], lam_col[:], -1.0, 0.0, ALU.mult, ALU.add)

        scores = []
        for s in range(2):
            grouped = sb.tile([P, Q, PACK], BF16, name=f"grouped{s}", align_bytes=64)
            dst = grouped[:].rearrange("p (c i) t -> p c t i", i=4)
            src = raw[s][:].rearrange("p t (c i) -> p c t i", i=4)
            if s == 0:
                nc.vector.tensor_copy(out=dst[:, :16], in_=src[:, :16])
                nc.scalar.activation(dst[:, 16:], src[:, 16:], COPY)
            else:
                nc.vector.tensor_copy(out=dst, in_=src)
            codes = sb.tile([P, Q], U32, name=f"codes{s}", align_bytes=64)
            scale = sb.tile([P, Q], U8, name=f"scale{s}", align_bytes=64)
            nc.vector.quantize_mx(
                out=codes[:].bitcast(FP8X4), scales=scale[:], in_=grouped[:].rearrange("p w j -> p (w j)")
            )
            score = sb.tile([P, T], F32, name=f"score{s}")
            scores.append(score)
            for n in (0, 1, 2, 3) if s == 0 else (2, 3, 0, 1):
                cols = slice(n * N_PASS, (n + 1) * N_PASS)
                h, c0 = divmod(n * N_PASS, T // 2)
                bank = ps.tile([P, N_PASS], F32, name=f"bank{s}_{n}", tag=f"bank{n + 2 * s if s == 0 or n < 2 else n + 2}")
                nc.tensor.matmul_mx(
                    out=bank[:],
                    lhsT=codes[:].bitcast(FP8X4),
                    lhsT_scale=scale[:],
                    rhs=key_words[h][:, c0 : c0 + N_PASS].bitcast(FP8X4),
                    rhs_scale=key_scale[:, cols],
                    start=True,
                    stop=True,
                )
                if s == 0 and n < 3:
                    nc.scalar.activation(score[:, cols], bank[:], COPY)
                else:
                    nc.vector.tensor_copy(out=score[:, cols], in_=bank[:])
        a, b = scores
        old_sb = sb.tile([P, T], F32, name="old_sb", tag="stage1")
        nc.sync.dma_start(out=old_sb[:], in_=old)

        def entries(lst, start, count):
            return lst[:, start // 16 : (start + count) // 16]

        ga = sb.tile([P, 2 * HALF], F32, name="ga")
        gb = [sb.tile([P, 2 * HALF], F32, name=f"gb{c}") for c in range(2)]
        top = sb.tile([P, 2, HALF], F32, name="top")
        late = [sb.tile([P, HALF], F32, name=f"late{s}") for s in range(2)]
        term = [sb.tile([P, HALF], F32, name=f"term{s}") for s in range(2)]

        def pairs(tile):
            return tile[:].rearrange("p (s i) -> p s i", s=2)

        def look_scalar(dst, window, lst, c):
            nc.scalar.activation(dst, window[:].indirect(entries(lst, c * HALF, HALF)), COPY)

        look_scalar(ga[:, :HALF], a, list1, 0)
        look_scalar(ga[:, HALF:], a, list2, 0)
        look_scalar(gb[0][:, HALF:], b, list1, 0)
        nc.vector.tensor_copy(gb[0][:, :HALF], b[:].indirect(entries(list2, 0, HALF)))
        look_scalar(gb[1][:, :HALF], b, list2, 1)
        look_scalar(gb[1][:, HALF:], b, list1, 1)
        pieces = [slice(p * PIECE, (p + 1) * PIECE) for p in range(2)]
        for cols in pieces:
            nc.vector.tensor_tensor(top[:, :, cols], pairs(ga)[:, :, cols], pairs(gb[0])[:, :, cols], ALU.max)
        for cols in pieces:
            nc.vector.tensor_tensor(top[:, 0, cols], top[:, 0, cols], top[:, 1, cols], ALU.subtract)
        look_scalar(ga[:, :HALF], a, list1, 1)
        look_scalar(ga[:, HALF:], a, list2, 1)
        for p, (cols, factor) in enumerate(zip(pieces, (lam_col, lam_neg))):
            nc.vector.tensor_tensor(
                f1[:].indirect(entries(list1, p * PIECE, PIECE)), top[:, 0, cols], lam_wide[:], ALU.mult
            )
            for part in [slice(0, HALF)] if p == 0 else pieces:
                nc.vector.tensor_tensor(late[p][:, part], pairs(ga)[:, p, part], pairs(gb[1])[:, p, part], ALU.max)
                nc.scalar.activation(term[p][:, part], late[p][:, part], COPY, scale=factor[:, 0:1])
        nc.vector.tensor_tensor(f1[:].indirect(entries(list1, HALF, HALF)), term[0][:], term[1][:], ALU.add)

        f2 = sb.tile([P, T], F32, name="f2")
        nc.vector.tensor_tensor(f2[:], f1[:], old_sb[:], ALU.add)

        res = [sb.tile([P, HALF], F32, name=f"res{c}") for c in range(2)]
        nc.vector.tensor_copy(res[0][:], f2[:].indirect(entries(list3, 0, HALF)))
        nc.sync.dma_start(out=out[:, 0:HALF], in_=res[0][:])
        look_scalar(res[1][:], f2, list3, 1)
        nc.scalar.dma_start(out=out[:, HALF:], in_=res[1][:])
